import numpy as np
import ml_dtypes


def mxq(x, axis, fmt="e4m3"):
    dtype, down = {"e4m3": (ml_dtypes.float8_e4m3fn, 7), "e5m2": (ml_dtypes.float8_e5m2, 14)}[fmt]
    v = np.moveaxis(np.asarray(x, np.float32).astype(ml_dtypes.bfloat16).astype(np.float64), axis, -1)
    blocks = v.reshape(v.shape[:-1] + (-1, 32))
    amax = np.abs(blocks).max(-1, keepdims=True)
    byte = np.maximum(np.where(amax > 0, np.frexp(amax)[1] - 1 + 127, 0) - down, 1)
    scale = np.exp2(byte - 127.0)
    codes = (blocks / scale).astype(np.float32).astype(dtype).astype(np.float64)
    return np.moveaxis((codes * scale).reshape(v.shape), -1, axis)


WIDE = False


def mx_kscale(k):
    if not WIDE:
        return np.ones(k)
    levels = np.array([10, -10, 5, -5, 0])
    if k % 512:
        return np.exp2(np.random.permutation(np.resize(levels, k // 32))).repeat(32)
    a = np.empty((k // 512, 16))
    for p in range(k // 512):
        a[p, :8] = np.random.permutation(np.resize(levels, 8))
        for g in range(8):
            far = levels[np.abs(levels - a[p, g]) >= 10]
            a[p, g + 8] = far[np.random.randint(len(far))]
    return np.exp2(a.ravel()).repeat(32)


def f64(x):
    return np.asarray(x).astype(np.float64)


def striped(idx):
    return np.tile(np.asarray(idx).reshape(-1, 16).T, (8, 1)).astype(np.uint16)


def unstriped(offs):
    return offs[:16].T.reshape(-1).astype(np.int64)


def bf(x):
    return np.asarray(x, np.float32).astype(ml_dtypes.bfloat16)


def planes(Y):
    r, m = Y.shape
    b = f64(bf(Y)).reshape(r // 32, 32, m)
    amax = np.abs(b).max(1)
    byte = np.clip(np.where(amax > 0, np.frexp(amax)[1] - 1 + 127 - 7, 1), 1, 254)
    codes = (b * np.exp2(127.0 - byte)[:, None, :]).reshape(r, m).astype(np.float32).astype(ml_dtypes.float8_e4m3fn).view(np.uint8)
    words = codes.reshape(r // 512, 128, 4, m).transpose(0, 1, 3, 2)
    return np.ascontiguousarray(words), np.ascontiguousarray(byte.astype(np.uint8).reshape(r // 512, 16, m))


D, T, J, Q, E = 512, 2048, 512, 256, 512


def setup_inputs():
    n = np.random.standard_normal
    idx = np.random.permutation(T)[:J]
    idx2 = np.random.permutation(T)[:J]
    fd = mx_kscale(D)
    fj = mx_kscale(J)
    return {
        "query": (n((D, Q)) * 0.4 / np.sqrt(D) * fd[:, None]).astype(np.float32),
        "keys": (n((D, T)) / fd[:, None]).astype(np.float32),
        "vals": (n((E, T))).astype(np.float32),
        "ka": (np.random.uniform(0.5, 1.0, (1, J))).astype(np.float32),
        "kb": (np.random.uniform(0.2, 0.7, (1, J))).astype(np.float32),
        "va": (np.random.uniform(0.5, 1.0, (1, J))).astype(np.float32),
        "vb": (np.random.uniform(0.2, 0.7, (1, J))).astype(np.float32),
        "size": (np.random.uniform(0.5, 2.0, (1, J)) * fj).astype(np.float32),
        "vsc": (np.random.uniform(0.5, 2.0, (J, 1)) / fj[:, None]).astype(np.float32),
        "offs": striped(idx),
        "offs2": striped(idx2),
    }


def reference(query, keys, vals, ka, kb, va, vb, size, vsc, offs, offs2):
    idx = unstriped(offs)
    idx2 = unstriped(offs2)
    km = f64(keys)[:, idx] * f64(ka) + f64(keys)[:, idx2] * f64(kb)
    vm = f64(vals)[:, idx] * f64(va) + f64(vals)[:, idx2] * f64(vb)
    queryq = mxq(f64(query), 0, "e4m3")
    kmq = mxq(km, 0, "e4m3")
    a = queryq.T @ kmq
    p = np.exp(a - np.max(a, axis=1, keepdims=True))
    w = p * f64(size) / np.sum(p, axis=1, keepdims=True)
    wt = w.T
    vt = vm.T
    vv = vt * f64(vsc)
    vvq = mxq(vv, 0, "e4m3")
    wtq = mxq(wt, 0, "e4m3")
    o = vvq.T @ wtq
    words, scales = planes(o)
    return o, words, scales

@@ -1,0 +1,221 @@
+from contextlib import ExitStack
+
+import concourse.mybir as mybir
+from concourse.masks import make_identity
+
+F32 = mybir.dt.float32
+BF16 = mybir.dt.bfloat16
+I32 = mybir.dt.int32
+U32 = mybir.dt.uint32
+U16 = mybir.dt.uint16
+U8 = mybir.dt.uint8
+FP8X4 = mybir.dt.float8_e4m3fn_x4
+ALU = mybir.AluOpType
+ACT = mybir.ActivationFunctionType
+AX = mybir.AxisListType
+
+D, T, J, Q, E = 512, 2048, 512, 256, 512
+P = 128
+FLOPS = 2 * Q * J * D + 2 * E * Q * J
+
+
+def tile_attend_cachemerge_pl_kernel(tc, query, keys, vals, ka, kb, va, vb, size, vsc, offs, offs2, out_0, out_1, out_2):
+    nc = tc.nc
+    with ExitStack() as ctx:
+        lists = ctx.enter_context(tc.tile_pool(name="lists", bufs=1))
+        keep = ctx.enter_context(tc.tile_pool(name="keep", bufs=1))
+        ring = ctx.enter_context(tc.tile_pool(name="ring", bufs=4))
+        turn = ctx.enter_context(tc.psum_pool(name="turn", bufs=6))
+        prod = ctx.enter_context(tc.psum_pool(name="prod", bufs=2))
+
+        kept = lists.tile([P, J // 16], U16, name="kept")
+        evicted = lists.tile([P, J // 16], U16, name="evicted")
+        key_pool = [keep.tile([P, T], F32, name="key_pool%d" % g) for g in range(4)]
+        val_pool = [keep.tile([P, T], F32, name="val_pool%d" % t) for t in range(4)]
+        q_raw = keep.tile([P, 4, Q], F32, name="q_raw")
+        cols = {}
+        for name in ("ka", "kb", "va", "vb", "size", "vsc"):
+            cols[name] = keep.tile([P, 4], F32, name="col_" + name)
+
+        def load_col(name, src):
+            nc.scalar.dma_start(out=cols[name][:], in_=src)
+
+        val_rows = vals.rearrange("(p t) n -> p t n", t=4)
+        nc.sync.dma_start(kept[:], offs)
+        load_col("ka", ka.rearrange("o (p c) -> (o p) c", c=4))
+        nc.sync.dma_start(out=key_pool[0][:], in_=keys[0:P, :])
+        load_col("kb", kb.rearrange("o (p c) -> (o p) c", c=4))
+        nc.sync.dma_start(evicted[:], offs2)
+        load_col("va", va.rearrange("o (p c) -> (o p) c", c=4))
+        load_col("vb", vb.rearrange("o (p c) -> (o p) c", c=4))
+        load_col("vsc", vsc.rearrange("(p c) o -> p (c o)", c=4))
+        nc.sync.dma_start(out=cols["size"][:], in_=size.rearrange("o (p c) -> (o p) c", c=4))
+        nc.sync.dma_start(out=key_pool[1][:], in_=keys[P : 2 * P, :])
+        nc.sync.dma_start(out=key_pool[2][:], in_=keys[2 * P : 3 * P, :])
+        nc.sync.dma_start(out=q_raw[:], in_=query.rearrange("(p t) q -> p t q", t=4))
+        nc.sync.dma_start(out=key_pool[3][:], in_=keys[3 * P : 4 * P, :])
+        for t in range(4):
+            nc.sync.dma_start(out=val_pool[t][:], in_=val_rows[:, t, :])
+
+        ident = keep.tile([P, P], F32, name="ident")
+        make_identity(nc, ident[:])
+
+        def spread(col, name, pairs):
+            bank = turn.tile([P, 4, P], F32, name="bank")
+            for c in range(4):
+                nc.tensor.transpose(bank[:, c, :], col[:, c : c + 1].to_broadcast([P, P]), ident[:])
+            row = keep.tile([P, J], F32, name=name)
+            if pairs:
+                nc.scalar.copy(out=row[:].rearrange("p (u n e) -> p u n e", u=2, e=2), in_=bank[:].rearrange("p (u e) n -> p u n e", u=2))
+            else:
+                nc.scalar.copy(out=row[:].rearrange("p (n c) -> p n c", c=4), in_=bank[:].rearrange("p c n -> p n c"))
+            return row
+
+        def gather(pool_tile, offsets, share):
+            picked = ring.tile([P, J], F32, name="picked")
+            nc.vector.tensor_tensor(picked[:], pool_tile[:].indirect(offsets[:]), share[:], ALU.mult)
+            return picked
+
+        def turn_and_add(bank, picked, columns, first):
+            for c in range(4):
+                nc.tensor.matmul(bank[:, c, :], picked[:, columns(c)], ident[:], start=(first and c == 0), stop=(not first and c == 3), is_transpose=True)
+
+        def quantize(src, width, name):
+            codes = keep.tile([P, width], U32, name=name + "_codes", align_bytes=64)
+            scales = keep.tile([P, width], U8, name=name + "_scales", align_bytes=64)
+            nc.vector.quantize_mx(out=codes[:].bitcast(FP8X4), scales=scales[:], in_=src)
+            return codes, scales
+
+        ka_row = spread(cols["ka"], "ka_row", False)
+        kb_row = spread(cols["kb"], "kb_row", False)
+
+        km_rows = keep.tile([P, 4, 2, P, 2], BF16, name="km_rows", align_bytes=64)
+
+        def key_block(g):
+            bank = turn.tile([P, 4, P], F32, name="bank")
+            blocks = lambda c: slice(c * P, (c + 1) * P)
+            turn_and_add(bank, gather(key_pool[g], kept, ka_row), blocks, True)
+            turn_and_add(bank, gather(key_pool[g], evicted, kb_row), blocks, False)
+            nc.scalar.copy(out=km_rows[:, :, :, 32 * g : 32 * (g + 1), :], in_=bank[:].rearrange("j c (r u e) -> j c u r e", u=2, e=2))
+
+        key_block(0)
+        q_words = keep.tile([P, Q, 4], BF16, name="q_words", align_bytes=64)
+        nc.scalar.copy(out=q_words[:], in_=q_raw[:].rearrange("p t q -> p q t"))
+        key_block(1)
+        q_codes, q_scales = quantize(q_words[:].rearrange("p q t -> p (q t)"), Q, "q")
+        va_col = keep.tile([P, 4], F32, name="va_col")
+        vb_col = keep.tile([P, 4], F32, name="vb_col")
+        nc.vector.tensor_tensor(va_col[:], cols["va"][:], cols["vsc"][:], ALU.mult)
+        nc.vector.tensor_tensor(vb_col[:], cols["vb"][:], cols["vsc"][:], ALU.mult)
+        key_block(2)
+        va_row = spread(va_col, "va_row", False)
+        vb_row = spread(vb_col, "vb_row", False)
+        size_row = spread(cols["size"], "size_row", True)
+        key_block(3)
+
+        km_pairs = km_rows[:].rearrange("j c u p e -> j (c u p e)").bitcast(F32)
+        km_words = keep.tile([P, J * 4], BF16, name="km_words", align_bytes=64)
+        for b in range(2):
+            bank = turn.tile([P, 2, 2, P], F32, name="bank")
+            for c in range(2):
+                for u in range(2):
+                    at = ((2 * b + c) * 2 + u) * P
+                    nc.tensor.transpose(bank[:, c, u, :], km_pairs[:, at : at + P], ident[:])
+            nc.scalar.copy(
+                out=km_words[:, 1024 * b : 1024 * (b + 1)].bitcast(F32).rearrange("p (c j u) -> p c j u", c=2, u=2),
+                in_=bank[:].rearrange("p c u j -> p c j u"),
+            )
+
+        v_words = []
+
+        def value_half(t, bank, first):
+            steps = lambda s: slice(s, J, 4)
+            if first:
+                turn_and_add(bank, gather(val_pool[t], kept, va_row), steps, True)
+            else:
+                turn_and_add(bank, gather(val_pool[t], evicted, vb_row), steps, False)
+                words = keep.tile([P, P, 4], BF16, name="v_words%d" % t, align_bytes=64)
+                nc.scalar.copy(out=words[:], in_=bank[:].rearrange("p s e -> p e s"))
+                v_words.append(words)
+
+        v_banks = [turn.tile([P, 4, P], F32, name="bank") for t in range(2)]
+        value_half(0, v_banks[0], True)
+        value_half(0, v_banks[0], False)
+        value_half(1, v_banks[1], True)
+
+        km_codes, km_scales = quantize(km_words[:], J, "km")
+        scores = [prod.tile([P, J], F32, name="product") for h in range(2)]
+        for h in range(2):
+            rows = slice(h * P, (h + 1) * P)
+            nc.tensor.matmul_mx(out=scores[h][:], lhsT=q_codes[:, rows].bitcast(FP8X4), lhsT_scale=q_scales[:, rows], rhs=km_codes[:].bitcast(FP8X4), rhs_scale=km_scales[:], start=True, stop=True)
+
+        value_half(1, v_banks[1], False)
+
+        weights = []
+        sums = []
+        for h in range(2):
+            neg_max = keep.tile([P, 1], F32, name="neg_max%d" % h)
+            nc.vector.tensor_reduce(out=neg_max[:], in_=scores[h][:], axis=AX.X, op=ALU.max, negate=True)
+            p_rows = keep.tile([P, J], F32, name="p_rows%d" % h)
+            total = keep.tile([P, 1], F32, name="total%d" % h)
+            nc.scalar.activation(out=p_rows[:].rearrange("q (u n e) -> q u n e", u=2, e=2), in_=scores[h][:].rearrange("q (n u e) -> q u n e", u=2, e=2), func=ACT.Exp, bias=neg_max[:], scale=1.0, accum_out=total[:])
+            weights.append(p_rows)
+            sums.append(total)
+
+        v_banks.append(turn.tile([P, 4, P], F32, name="bank"))
+        value_half(2, v_banks[2], True)
+
+        inverse = []
+        for h in range(2):
+            inv = keep.tile([P, 1], F32, name="inverse%d" % h)
+            nc.vector.reciprocal(inv[:], sums[h][:])
+            inverse.append(inv)
+        w_bank = turn.tile([P, 2, 2, P], F32, name="bank")
+        for h in range(2):
+            w_rows = keep.tile([P, J], BF16, name="w_rows%d" % h, align_bytes=64)
+            nc.vector.scalar_tensor_tensor(out=w_rows[:], in0=weights[h][:], scalar=inverse[h][:], in1=size_row[:], op0=ALU.mult, op1=ALU.mult)
+            w_pairs = w_rows[:].bitcast(F32)
+            for u in range(2):
+                nc.tensor.transpose(w_bank[:, h, u, :], w_pairs[:, u * P : (u + 1) * P], ident[:])
+        w_words = keep.tile([P, Q * 4], BF16, name="w_words", align_bytes=64)
+        nc.scalar.copy(out=w_words[:].bitcast(F32).rearrange("p (h q u) -> p h q u", h=2, u=2), in_=w_bank[:].rearrange("p h u q -> p h q u"))
+
+        value_half(2, v_banks[2], False)
+        v_banks.append(turn.tile([P, 4, P], F32, name="bank"))
+        value_half(3, v_banks[3], True)
+        value_half(3, v_banks[3], False)
+
+        w_codes, w_scales = quantize(w_words[:], Q, "w")
+        result = [prod.tile([P, 4, P], F32, name="product") for h in range(2)]
+        out_rows = keep.tile([P, 4, Q], F32, name="out_rows")
+        out_view = out_0.rearrange("(p t) q -> p t q", t=4)
+
+        def product(t):
+            v_codes, v_scales = quantize(v_words[t][:].rearrange("p e s -> p (e s)"), P, "v%d" % t)
+            for h in range(2):
+                rows = slice(h * P, (h + 1) * P)
+                nc.tensor.matmul_mx(out=result[h][:, t, :], lhsT=v_codes[:].bitcast(FP8X4), lhsT_scale=v_scales[:], rhs=w_codes[:, rows].bitcast(FP8X4), rhs_scale=w_scales[:, rows], start=True, stop=True)
+
+        for t in range(3):
+            product(t)
+        for h in range(2):
+            nc.scalar.copy(out=out_rows[:, 0:3, h * P : (h + 1) * P], in_=result[h][:, 0:3, :])
+        nc.sync.dma_start(out=out_view[:, 0:3, :], in_=out_rows[:, 0:3, :])
+        product(3)
+
+        halves = [keep.tile([P, P, 4], BF16, name="out_words%d" % h, align_bytes=64) for h in range(2)]
+        nc.scalar.copy(out=halves[0][:], in_=result[0][:].rearrange("p t q -> p q t"))
+        nc.vector.tensor_copy(out=halves[1][:], in_=result[1][:].rearrange("p t q -> p q t"))
+        last = keep.tile([P, Q], F32, name="last_rows")
+        for h in range(2):
+            nc.scalar.copy(out=last[:, h * P : (h + 1) * P], in_=result[h][:, 3, :])
+        nc.scalar.dma_start(out=out_view[:, 3, :], in_=last[:])
+        o_codes = keep.tile([P, Q], U32, name="o_codes", align_bytes=64)
+        o_scales = keep.tile([P, Q], U8, name="o_scales", align_bytes=64)
+        for h in range(2):
+            rows = slice(h * P, (h + 1) * P)
+            nc.vector.quantize_mx(out=o_codes[:, rows].bitcast(FP8X4), scales=o_scales[:, rows], in_=halves[h][:].rearrange("p q t -> p (q t)"))
+        nc.sync.dma_start(out=out_1[0].rearrange("p q r -> p (q r)").bitcast(I32), in_=o_codes[:].bitcast(I32))
+        for quad in range(4):
+            queue = nc.sync if quad < 2 else nc.scalar
+            queue.dma_start(out=out_2[0, 4 * quad : 4 * quad + 4, :].bitcast(I32), in_=o_scales[32 * quad : 32 * quad + 4, :].bitcast(I32))

@@ -24,55 +24,55 @@ def tile_attend_cachemerge_pl_kernel(tc, query, keys, vals, ka, kb, va, vb, size
     with ExitStack() as ctx:
         lists = ctx.enter_context(tc.tile_pool(name="lists", bufs=1))
         keep = ctx.enter_context(tc.tile_pool(name="keep", bufs=1))
-        ring = ctx.enter_context(tc.tile_pool(name="ring", bufs=4))
         turn = ctx.enter_context(tc.psum_pool(name="turn", bufs=6))
         prod = ctx.enter_context(tc.psum_pool(name="prod", bufs=2))
 
+        def sbuf(shape, dtype, name, slot=None):
+            return keep.tile(shape, dtype, name=name, tag=slot or name, align_bytes=64)
+
         kept = lists.tile([P, J // 16], U16, name="kept")
         evicted = lists.tile([P, J // 16], U16, name="evicted")
-        key_pool = [keep.tile([P, T], F32, name="key_pool%d" % g) for g in range(4)]
-        val_pool = [keep.tile([P, T], F32, name="val_pool%d" % t) for t in range(4)]
-        q_raw = keep.tile([P, 4, Q], F32, name="q_raw")
-        cols = {}
-        for name in ("ka", "kb", "va", "vb", "size", "vsc"):
-            cols[name] = keep.tile([P, 4], F32, name="col_" + name)
+        key_pool = [sbuf([P, T], F32, "key_pool%d" % g) for g in range(4)]
+        val_pool = [sbuf([P, T], F32, "val_pool%d" % t) for t in range(4)]
+        q_raw = sbuf([P, 4, Q], F32, "q_raw")
+        cols = {name: sbuf([P, 4], F32, "col_" + name) for name in ("ka", "kb", "va", "vb", "size", "vsc")}
 
-        def load_col(name, src):
-            nc.scalar.dma_start(out=cols[name][:], in_=src)
+        def load_col(queue, name, src):
+            queue.dma_start(out=cols[name][:], in_=src.rearrange("o (p c) -> (o p) c", c=4))
 
         val_rows = vals.rearrange("(p t) n -> p t n", t=4)
         nc.sync.dma_start(kept[:], offs)
-        load_col("ka", ka.rearrange("o (p c) -> (o p) c", c=4))
+        load_col(nc.scalar, "ka", ka)
         nc.sync.dma_start(out=key_pool[0][:], in_=keys[0:P, :])
-        load_col("kb", kb.rearrange("o (p c) -> (o p) c", c=4))
+        load_col(nc.scalar, "kb", kb)
         nc.sync.dma_start(evicted[:], offs2)
-        load_col("va", va.rearrange("o (p c) -> (o p) c", c=4))
-        load_col("vb", vb.rearrange("o (p c) -> (o p) c", c=4))
-        load_col("vsc", vsc.rearrange("(p c) o -> p (c o)", c=4))
-        nc.sync.dma_start(out=cols["size"][:], in_=size.rearrange("o (p c) -> (o p) c", c=4))
-        nc.sync.dma_start(out=key_pool[1][:], in_=keys[P : 2 * P, :])
-        nc.sync.dma_start(out=key_pool[2][:], in_=keys[2 * P : 3 * P, :])
-        nc.sync.dma_start(out=q_raw[:], in_=query.rearrange("(p t) q -> p t q", t=4))
-        nc.sync.dma_start(out=key_pool[3][:], in_=keys[3 * P : 4 * P, :])
+        load_col(nc.scalar, "va", va)
+        load_col(nc.scalar, "vb", vb)
+        nc.scalar.dma_start(out=cols["vsc"][:], in_=vsc.rearrange("(p c) o -> p (c o)", c=4))
+        load_col(nc.sync, "size", size)
+        for g in range(1, 4):
+            nc.sync.dma_start(out=key_pool[g][:], in_=keys[g * P : (g + 1) * P, :])
         for t in range(4):
             nc.sync.dma_start(out=val_pool[t][:], in_=val_rows[:, t, :])
+            if t == 1:
+                nc.sync.dma_start(out=q_raw[:], in_=query.rearrange("(p t) q -> p t q", t=4))
 
-        ident = keep.tile([P, P], F32, name="ident")
+        ident = sbuf([P, P], F32, "ident")
         make_identity(nc, ident[:])
 
         def spread(col, name, pairs):
             bank = turn.tile([P, 4, P], F32, name="bank")
             for c in range(4):
                 nc.tensor.transpose(bank[:, c, :], col[:, c : c + 1].to_broadcast([P, P]), ident[:])
-            row = keep.tile([P, J], F32, name=name)
+            row = sbuf([P, J], F32, name)
             if pairs:
                 nc.scalar.copy(out=row[:].rearrange("p (u n e) -> p u n e", u=2, e=2), in_=bank[:].rearrange("p (u e) n -> p u n e", u=2))
             else:
                 nc.scalar.copy(out=row[:].rearrange("p (n c) -> p n c", c=4), in_=bank[:].rearrange("p c n -> p n c"))
             return row
 
-        def gather(pool_tile, offsets, share):
-            picked = ring.tile([P, J], F32, name="picked")
+        def gather(pool_tile, offsets, share, name, slot=None):
+            picked = sbuf([P, J], F32, name, slot)
             nc.vector.tensor_tensor(picked[:], pool_tile[:].indirect(offsets[:]), share[:], ALU.mult)
             return picked
 
@@ -80,41 +80,34 @@ def tile_attend_cachemerge_pl_kernel(tc, query, keys, vals, ka, kb, va, vb, size
             for c in range(4):
                 nc.tensor.matmul(bank[:, c, :], picked[:, columns(c)], ident[:], start=(first and c == 0), stop=(not first and c == 3), is_transpose=True)
 
-        def quantize(src, width, name):
-            codes = keep.tile([P, width], U32, name=name + "_codes", align_bytes=64)
-            scales = keep.tile([P, width], U8, name=name + "_scales", align_bytes=64)
-            nc.vector.quantize_mx(out=codes[:].bitcast(FP8X4), scales=scales[:], in_=src)
-            return codes, scales
+        def quantize(codes, scales, src):
+            nc.vector.quantize_mx(out=codes.bitcast(FP8X4), scales=scales, in_=src)
 
         ka_row = spread(cols["ka"], "ka_row", False)
         kb_row = spread(cols["kb"], "kb_row", False)
+        va_col = sbuf([P, 4], F32, "va_col")
+        vb_col = sbuf([P, 4], F32, "vb_col")
+        nc.gpsimd.tensor_tensor(va_col[:], cols["va"][:], cols["vsc"][:], ALU.mult)
+        nc.gpsimd.tensor_tensor(vb_col[:], cols["vb"][:], cols["vsc"][:], ALU.mult)
 
-        km_rows = keep.tile([P, 4, 2, P, 2], BF16, name="km_rows", align_bytes=64)
+        km_rows = sbuf([P, 4, 2, P, 2], BF16, "km_rows")
 
         def key_block(g):
             bank = turn.tile([P, 4, P], F32, name="bank")
             blocks = lambda c: slice(c * P, (c + 1) * P)
-            turn_and_add(bank, gather(key_pool[g], kept, ka_row), blocks, True)
-            turn_and_add(bank, gather(key_pool[g], evicted, kb_row), blocks, False)
+            turn_and_add(bank, gather(key_pool[g], kept, ka_row, "ka%d" % g), blocks, True)
+            turn_and_add(bank, gather(key_pool[g], evicted, kb_row, "kb%d" % g), blocks, False)
             nc.scalar.copy(out=km_rows[:, :, :, 32 * g : 32 * (g + 1), :], in_=bank[:].rearrange("j c (r u e) -> j c u r e", u=2, e=2))
 
         key_block(0)
-        q_words = keep.tile([P, Q, 4], BF16, name="q_words", align_bytes=64)
-        nc.scalar.copy(out=q_words[:], in_=q_raw[:].rearrange("p t q -> p q t"))
-        key_block(1)
-        q_codes, q_scales = quantize(q_words[:].rearrange("p q t -> p (q t)"), Q, "q")
-        va_col = keep.tile([P, 4], F32, name="va_col")
-        vb_col = keep.tile([P, 4], F32, name="vb_col")
-        nc.vector.tensor_tensor(va_col[:], cols["va"][:], cols["vsc"][:], ALU.mult)
-        nc.vector.tensor_tensor(vb_col[:], cols["vb"][:], cols["vsc"][:], ALU.mult)
-        key_block(2)
         va_row = spread(va_col, "va_row", False)
         vb_row = spread(vb_col, "vb_row", False)
         size_row = spread(cols["size"], "size_row", True)
-        key_block(3)
+        for g in range(1, 4):
+            key_block(g)
 
         km_pairs = km_rows[:].rearrange("j c u p e -> j (c u p e)").bitcast(F32)
-        km_words = keep.tile([P, J * 4], BF16, name="km_words", align_bytes=64)
+        km_words = sbuf([P, J * 4], BF16, "km_words")
         for b in range(2):
             bank = turn.tile([P, 2, 2, P], F32, name="bank")
             for c in range(2):
@@ -126,95 +119,103 @@ def tile_attend_cachemerge_pl_kernel(tc, query, keys, vals, ka, kb, va, vb, size
                 in_=bank[:].rearrange("p c u j -> p c j u"),
             )
 
-        v_words = []
+        v_words = [sbuf([P, 2 * J], BF16, "v_words%d" % a) for a in range(2)]
+        steps = lambda s: slice(s, J, 4)
 
-        def value_half(t, bank, first):
-            steps = lambda s: slice(s, J, 4)
-            if first:
-                turn_and_add(bank, gather(val_pool[t], kept, va_row), steps, True)
-            else:
-                turn_and_add(bank, gather(val_pool[t], evicted, vb_row), steps, False)
-                words = keep.tile([P, P, 4], BF16, name="v_words%d" % t, align_bytes=64)
-                nc.scalar.copy(out=words[:], in_=bank[:].rearrange("p s e -> p e s"))
-                v_words.append(words)
+        def value_kept(t):
+            bank = turn.tile([P, 4, P], F32, name="bank")
+            turn_and_add(bank, gather(val_pool[t], kept, va_row, "va%d" % t), steps, True)
+            return bank
 
-        v_banks = [turn.tile([P, 4, P], F32, name="bank") for t in range(2)]
-        value_half(0, v_banks[0], True)
-        value_half(0, v_banks[0], False)
-        value_half(1, v_banks[1], True)
+        def value_evicted(t, bank, slot=None):
+            turn_and_add(bank, gather(val_pool[t], evicted, vb_row, "vb%d" % t, slot), steps, False)
+            words = v_words[t // 2][:, (t % 2) * J : (t % 2 + 1) * J]
+            nc.scalar.copy(out=words.rearrange("p (e s) -> p e s", s=4), in_=bank[:].rearrange("p s e -> p e s"))
 
-        km_codes, km_scales = quantize(km_words[:], J, "km")
+        for t in range(2):
+            value_evicted(t, value_kept(t))
+
+        km_codes = sbuf([P, J], U32, "km_codes", "val_pool1")
+        km_scales = sbuf([P, J], U8, "km_scales")
+        quantize(km_codes[:], km_scales[:], km_words[:])
+        q_words = sbuf([P, Q, 4], BF16, "q_words")
+        nc.scalar.copy(out=q_words[:], in_=q_raw[:].rearrange("p t q -> p q t"))
+        q_codes = sbuf([P, Q], U32, "q_codes")
+        q_scales = sbuf([P, Q], U8, "q_scales")
+        quantize(q_codes[:], q_scales[:], q_words[:].rearrange("p q t -> p (q t)"))
         scores = [prod.tile([P, J], F32, name="product") for h in range(2)]
         for h in range(2):
             rows = slice(h * P, (h + 1) * P)
             nc.tensor.matmul_mx(out=scores[h][:], lhsT=q_codes[:, rows].bitcast(FP8X4), lhsT_scale=q_scales[:, rows], rhs=km_codes[:].bitcast(FP8X4), rhs_scale=km_scales[:], start=True, stop=True)
 
-        value_half(1, v_banks[1], False)
+        value_evicted(2, value_kept(2))
 
         weights = []
         sums = []
         for h in range(2):
-            neg_max = keep.tile([P, 1], F32, name="neg_max%d" % h)
+            neg_max = sbuf([P, 1], F32, "neg_max%d" % h, "val_pool2" if h == 0 else None)
             nc.vector.tensor_reduce(out=neg_max[:], in_=scores[h][:], axis=AX.X, op=ALU.max, negate=True)
-            p_rows = keep.tile([P, J], F32, name="p_rows%d" % h)
-            total = keep.tile([P, 1], F32, name="total%d" % h)
+            p_rows = sbuf([P, J], F32, "p_rows%d" % h)
+            total = sbuf([P, 1], F32, "total%d" % h)
             nc.scalar.activation(out=p_rows[:].rearrange("q (u n e) -> q u n e", u=2, e=2), in_=scores[h][:].rearrange("q (n u e) -> q u n e", u=2, e=2), func=ACT.Exp, bias=neg_max[:], scale=1.0, accum_out=total[:])
             weights.append(p_rows)
             sums.append(total)
 
-        v_banks.append(turn.tile([P, 4, P], F32, name="bank"))
-        value_half(2, v_banks[2], True)
+        last_bank = value_kept(3)
 
         inverse = []
         for h in range(2):
-            inv = keep.tile([P, 1], F32, name="inverse%d" % h)
+            inv = sbuf([P, 1], F32, "inverse%d" % h, "va_row" if h == 0 else None)
             nc.vector.reciprocal(inv[:], sums[h][:])
             inverse.append(inv)
         w_bank = turn.tile([P, 2, 2, P], F32, name="bank")
         for h in range(2):
-            w_rows = keep.tile([P, J], BF16, name="w_rows%d" % h, align_bytes=64)
+            w_rows = sbuf([P, J], BF16, "w_rows%d" % h)
             nc.vector.scalar_tensor_tensor(out=w_rows[:], in0=weights[h][:], scalar=inverse[h][:], in1=size_row[:], op0=ALU.mult, op1=ALU.mult)
             w_pairs = w_rows[:].bitcast(F32)
             for u in range(2):
                 nc.tensor.transpose(w_bank[:, h, u, :], w_pairs[:, u * P : (u + 1) * P], ident[:])
-        w_words = keep.tile([P, Q * 4], BF16, name="w_words", align_bytes=64)
+        w_words = sbuf([P, Q * 4], BF16, "w_words")
         nc.scalar.copy(out=w_words[:].bitcast(F32).rearrange("p (h q u) -> p h q u", h=2, u=2), in_=w_bank[:].rearrange("p h u q -> p h q u"))
 
-        value_half(2, v_banks[2], False)
-        v_banks.append(turn.tile([P, 4, P], F32, name="bank"))
-        value_half(3, v_banks[3], True)
-        value_half(3, v_banks[3], False)
+        value_evicted(3, last_bank, "size_row")
 
-        w_codes, w_scales = quantize(w_words[:], Q, "w")
+        codes = sbuf([P, Q + E], U32, "codes", "val_pool3")
+        w_scales = sbuf([P, Q], U8, "w_scales")
+        v_scales = sbuf([P, E], U8, "v_scales")
+        quantize(codes[:, 0:Q], w_scales[:], w_words[:])
+        quantize(codes[:, Q : Q + 2 * P], v_scales[:, 0 : 2 * P], v_words[0][:])
+        quantize(codes[:, Q + 2 * P : Q + 3 * P], v_scales[:, 2 * P : 3 * P], v_words[1][:, 0:J])
         result = [prod.tile([P, 4, P], F32, name="product") for h in range(2)]
-        out_rows = keep.tile([P, 4, Q], F32, name="out_rows")
         out_view = out_0.rearrange("(p t) q -> p t q", t=4)
 
-        def product(t):
-            v_codes, v_scales = quantize(v_words[t][:].rearrange("p e s -> p (e s)"), P, "v%d" % t)
-            for h in range(2):
-                rows = slice(h * P, (h + 1) * P)
-                nc.tensor.matmul_mx(out=result[h][:, t, :], lhsT=v_codes[:].bitcast(FP8X4), lhsT_scale=v_scales[:], rhs=w_codes[:, rows].bitcast(FP8X4), rhs_scale=w_scales[:, rows], start=True, stop=True)
+        def product(t, h):
+            rows = slice(h * P, (h + 1) * P)
+            nc.tensor.matmul_mx(out=result[h][:, t, :], lhsT=codes[:, Q + t * P : Q + (t + 1) * P].bitcast(FP8X4), lhsT_scale=v_scales[:, t * P : (t + 1) * P], rhs=codes[:, rows].bitcast(FP8X4), rhs_scale=w_scales[:, rows], start=True, stop=True)
 
-        for t in range(3):
-            product(t)
+        out_rows = sbuf([P, 3, Q], F32, "out_rows")
         for h in range(2):
-            nc.scalar.copy(out=out_rows[:, 0:3, h * P : (h + 1) * P], in_=result[h][:, 0:3, :])
-        nc.sync.dma_start(out=out_view[:, 0:3, :], in_=out_rows[:, 0:3, :])
-        product(3)
+            for t in range(3):
+                product(t, h)
+        nc.vector.tensor_copy(out=out_rows[:, :, 0:P], in_=result[0][:, 0:3, :])
+        nc.scalar.copy(out=out_rows[:, :, P:Q], in_=result[1][:, 0:3, :])
+        nc.sync.dma_start(out=out_view[:, 0:3, :], in_=out_rows[:])
+        quantize(codes[:, Q + 3 * P : Q + 4 * P], v_scales[:, 3 * P : 4 * P], v_words[1][:, J : 2 * J])
+        for h in range(2):
+            product(3, h)
 
-        halves = [keep.tile([P, P, 4], BF16, name="out_words%d" % h, align_bytes=64) for h in range(2)]
-        nc.scalar.copy(out=halves[0][:], in_=result[0][:].rearrange("p t q -> p q t"))
-        nc.vector.tensor_copy(out=halves[1][:], in_=result[1][:].rearrange("p t q -> p q t"))
-        last = keep.tile([P, Q], F32, name="last_rows")
+        halves = [sbuf([P, P, 4], BF16, "out_words%d" % h) for h in range(2)]
+        nc.vector.tensor_copy(out=halves[0][:], in_=result[0][:].rearrange("p t q -> p q t"))
+        nc.scalar.copy(out=halves[1][:], in_=result[1][:].rearrange("p t q -> p q t"))
+        last = sbuf([P, Q], F32, "last_rows")
         for h in range(2):
             nc.scalar.copy(out=last[:, h * P : (h + 1) * P], in_=result[h][:, 3, :])
         nc.scalar.dma_start(out=out_view[:, 3, :], in_=last[:])
-        o_codes = keep.tile([P, Q], U32, name="o_codes", align_bytes=64)
-        o_scales = keep.tile([P, Q], U8, name="o_scales", align_bytes=64)
+        o_codes = sbuf([P, Q], U32, "o_codes")
+        o_scales = sbuf([P, Q], U8, "o_scales")
         for h in range(2):
             rows = slice(h * P, (h + 1) * P)
-            nc.vector.quantize_mx(out=o_codes[:, rows].bitcast(FP8X4), scales=o_scales[:, rows], in_=halves[h][:].rearrange("p q t -> p (q t)"))
+            quantize(o_codes[:, rows], o_scales[:, rows], halves[h][:].rearrange("p q t -> p (q t)"))
         nc.sync.dma_start(out=out_1[0].rearrange("p q r -> p (q r)").bitcast(I32), in_=o_codes[:].bitcast(I32))
         for quad in range(4):
             queue = nc.sync if quad < 2 else nc.scalar

@@ -52,24 +52,24 @@ def tile_attend_cachemerge_pl_kernel(tc, query, keys, vals, ka, kb, va, vb, size
         load_col(nc.sync, "size", size)
         for g in range(1, 4):
             nc.sync.dma_start(out=key_pool[g][:], in_=keys[g * P : (g + 1) * P, :])
+        nc.sync.dma_start(out=q_raw[:], in_=query.rearrange("(p t) q -> p t q", t=4))
         for t in range(4):
             nc.sync.dma_start(out=val_pool[t][:], in_=val_rows[:, t, :])
-            if t == 1:
-                nc.sync.dma_start(out=q_raw[:], in_=query.rearrange("(p t) q -> p t q", t=4))
 
         ident = sbuf([P, P], F32, "ident")
         make_identity(nc, ident[:])
 
-        def spread(col, name, pairs):
+        def spread(col, names, pairs):
             bank = turn.tile([P, 4, P], F32, name="bank")
             for c in range(4):
                 nc.tensor.transpose(bank[:, c, :], col[:, c : c + 1].to_broadcast([P, P]), ident[:])
-            row = sbuf([P, J], F32, name)
-            if pairs:
-                nc.scalar.copy(out=row[:].rearrange("p (u n e) -> p u n e", u=2, e=2), in_=bank[:].rearrange("p (u e) n -> p u n e", u=2))
-            else:
-                nc.scalar.copy(out=row[:].rearrange("p (n c) -> p n c", c=4), in_=bank[:].rearrange("p c n -> p n c"))
-            return row
+            rows = [sbuf([P, J], F32, name) for name in names]
+            for row in rows:
+                if pairs:
+                    nc.scalar.copy(out=row[:].rearrange("p (u n e) -> p u n e", u=2, e=2), in_=bank[:].rearrange("p (u e) n -> p u n e", u=2))
+                else:
+                    nc.scalar.copy(out=row[:].rearrange("p (n c) -> p n c", c=4), in_=bank[:].rearrange("p c n -> p n c"))
+            return rows
 
         def gather(pool_tile, offsets, share, name, slot=None):
             picked = sbuf([P, J], F32, name, slot)
@@ -83,8 +83,8 @@ def tile_attend_cachemerge_pl_kernel(tc, query, keys, vals, ka, kb, va, vb, size
         def quantize(codes, scales, src):
             nc.vector.quantize_mx(out=codes.bitcast(FP8X4), scales=scales, in_=src)
 
-        ka_row = spread(cols["ka"], "ka_row", False)
-        kb_row = spread(cols["kb"], "kb_row", False)
+        (ka_row,) = spread(cols["ka"], ["ka_row"], False)
+        (kb_row,) = spread(cols["kb"], ["kb_row"], False)
         va_col = sbuf([P, 4], F32, "va_col")
         vb_col = sbuf([P, 4], F32, "vb_col")
         nc.gpsimd.tensor_tensor(va_col[:], cols["va"][:], cols["vsc"][:], ALU.mult)
@@ -100,11 +100,17 @@ def tile_attend_cachemerge_pl_kernel(tc, query, keys, vals, ka, kb, va, vb, size
             nc.scalar.copy(out=km_rows[:, :, :, 32 * g : 32 * (g + 1), :], in_=bank[:].rearrange("j c (r u e) -> j c u r e", u=2, e=2))
 
         key_block(0)
-        va_row = spread(va_col, "va_row", False)
-        vb_row = spread(vb_col, "vb_row", False)
-        size_row = spread(cols["size"], "size_row", True)
+        va_rows = spread(va_col, ["va_row1", "va_row2", "va_row3"], False)
+        (vb_row,) = spread(vb_col, ["vb_row"], False)
+        (size_row,) = spread(cols["size"], ["size_row"], True)
         for g in range(1, 4):
             key_block(g)
+
+        q_words = sbuf([P, Q, 4], BF16, "q_words")
+        nc.scalar.copy(out=q_words[:], in_=q_raw[:].rearrange("p t q -> p q t"))
+        q_codes = sbuf([P, Q], U32, "q_codes", "ka_row")
+        q_scales = sbuf([P, Q], U8, "q_scales")
+        quantize(q_codes[:], q_scales[:], q_words[:].rearrange("p q t -> p (q t)"))
 
         km_pairs = km_rows[:].rearrange("j c u p e -> j (c u p e)").bitcast(F32)
         km_words = sbuf([P, J * 4], BF16, "km_words")
@@ -119,66 +125,63 @@ def tile_attend_cachemerge_pl_kernel(tc, query, keys, vals, ka, kb, va, vb, size
                 in_=bank[:].rearrange("p c u j -> p c j u"),
             )
 
-        v_words = [sbuf([P, 2 * J], BF16, "v_words%d" % a) for a in range(2)]
+        v_words = [sbuf([P, 2 * J], BF16, "v_words0")]
         steps = lambda s: slice(s, J, 4)
 
         def value_kept(t):
             bank = turn.tile([P, 4, P], F32, name="bank")
-            turn_and_add(bank, gather(val_pool[t], kept, va_row, "va%d" % t), steps, True)
+            turn_and_add(bank, gather(val_pool[t], kept, va_rows[max(t - 1, 0)], "va%d" % t), steps, True)
             return bank
 
         def value_evicted(t, bank, slot=None):
             turn_and_add(bank, gather(val_pool[t], evicted, vb_row, "vb%d" % t, slot), steps, False)
+
+        def value_words(t, bank):
             words = v_words[t // 2][:, (t % 2) * J : (t % 2 + 1) * J]
             nc.scalar.copy(out=words.rearrange("p (e s) -> p e s", s=4), in_=bank[:].rearrange("p s e -> p e s"))
 
         for t in range(2):
-            value_evicted(t, value_kept(t))
+            bank = value_kept(t)
+            value_evicted(t, bank)
+            value_words(t, bank)
 
-        km_codes = sbuf([P, J], U32, "km_codes", "val_pool1")
+        km_codes = sbuf([P, J], U32, "km_codes", "va_row1")
         km_scales = sbuf([P, J], U8, "km_scales")
         quantize(km_codes[:], km_scales[:], km_words[:])
-        q_words = sbuf([P, Q, 4], BF16, "q_words")
-        nc.scalar.copy(out=q_words[:], in_=q_raw[:].rearrange("p t q -> p q t"))
-        q_codes = sbuf([P, Q], U32, "q_codes")
-        q_scales = sbuf([P, Q], U8, "q_scales")
-        quantize(q_codes[:], q_scales[:], q_words[:].rearrange("p q t -> p (q t)"))
         scores = [prod.tile([P, J], F32, name="product") for h in range(2)]
         for h in range(2):
             rows = slice(h * P, (h + 1) * P)
             nc.tensor.matmul_mx(out=scores[h][:], lhsT=q_codes[:, rows].bitcast(FP8X4), lhsT_scale=q_scales[:, rows], rhs=km_codes[:].bitcast(FP8X4), rhs_scale=km_scales[:], start=True, stop=True)
 
-        value_evicted(2, value_kept(2))
+        third = value_kept(2)
+        value_evicted(2, third)
 
         weights = []
-        sums = []
+        totals = sbuf([P, 2], F32, "totals")
         for h in range(2):
-            neg_max = sbuf([P, 1], F32, "neg_max%d" % h, "val_pool2" if h == 0 else None)
+            neg_max = sbuf([P, 1], F32, "neg_max%d" % h, "va_row2" if h == 0 else None)
             nc.vector.tensor_reduce(out=neg_max[:], in_=scores[h][:], axis=AX.X, op=ALU.max, negate=True)
             p_rows = sbuf([P, J], F32, "p_rows%d" % h)
-            total = sbuf([P, 1], F32, "total%d" % h)
-            nc.scalar.activation(out=p_rows[:].rearrange("q (u n e) -> q u n e", u=2, e=2), in_=scores[h][:].rearrange("q (n u e) -> q u n e", u=2, e=2), func=ACT.Exp, bias=neg_max[:], scale=1.0, accum_out=total[:])
+            nc.scalar.activation(out=p_rows[:].rearrange("q (u n e) -> q u n e", u=2, e=2), in_=scores[h][:].rearrange("q (n u e) -> q u n e", u=2, e=2), func=ACT.Exp, bias=neg_max[:], scale=1.0, accum_out=totals[:, h : h + 1])
             weights.append(p_rows)
-            sums.append(total)
 
-        last_bank = value_kept(3)
-
-        inverse = []
-        for h in range(2):
-            inv = sbuf([P, 1], F32, "inverse%d" % h, "va_row" if h == 0 else None)
-            nc.vector.reciprocal(inv[:], sums[h][:])
-            inverse.append(inv)
+        v_words.append(sbuf([P, 2 * J], BF16, "v_words1", "neg_max1"))
+        value_words(2, third)
+        bank = value_kept(3)
+        inverse = sbuf([P, 2], F32, "inverse")
+        nc.vector.reciprocal(inverse[:], totals[:])
         w_bank = turn.tile([P, 2, 2, P], F32, name="bank")
         for h in range(2):
             w_rows = sbuf([P, J], BF16, "w_rows%d" % h)
-            nc.vector.scalar_tensor_tensor(out=w_rows[:], in0=weights[h][:], scalar=inverse[h][:], in1=size_row[:], op0=ALU.mult, op1=ALU.mult)
+            nc.vector.scalar_tensor_tensor(out=w_rows[:], in0=weights[h][:], scalar=inverse[:, h : h + 1], in1=size_row[:], op0=ALU.mult, op1=ALU.mult)
             w_pairs = w_rows[:].bitcast(F32)
             for u in range(2):
                 nc.tensor.transpose(w_bank[:, h, u, :], w_pairs[:, u * P : (u + 1) * P], ident[:])
         w_words = sbuf([P, Q * 4], BF16, "w_words")
         nc.scalar.copy(out=w_words[:].bitcast(F32).rearrange("p (h q u) -> p h q u", h=2, u=2), in_=w_bank[:].rearrange("p h u q -> p h q u"))
 
-        value_evicted(3, last_bank, "size_row")
+        value_evicted(3, bank, "p_rows0")
+        value_words(3, bank)
 
         codes = sbuf([P, Q + E], U32, "codes", "val_pool3")
         w_scales = sbuf([P, Q], U8, "w_scales")
@@ -197,10 +200,10 @@ def tile_attend_cachemerge_pl_kernel(tc, query, keys, vals, ka, kb, va, vb, size
         for h in range(2):
             for t in range(3):
                 product(t, h)
-        nc.vector.tensor_copy(out=out_rows[:, :, 0:P], in_=result[0][:, 0:3, :])
-        nc.scalar.copy(out=out_rows[:, :, P:Q], in_=result[1][:, 0:3, :])
-        nc.sync.dma_start(out=out_view[:, 0:3, :], in_=out_rows[:])
         quantize(codes[:, Q + 3 * P : Q + 4 * P], v_scales[:, 3 * P : 4 * P], v_words[1][:, J : 2 * J])
+        nc.scalar.copy(out=out_rows[:, :, 0:P], in_=result[0][:, 0:3, :])
+        nc.vector.tensor_copy(out=out_rows[:, :, P:Q], in_=result[1][:, 0:3, :])
+        nc.sync.dma_start(out=out_view[:, 0:3, :], in_=out_rows[:])
         for h in range(2):
             product(3, h)
 

from contextlib import ExitStack

import concourse.mybir as mybir
from concourse.masks import make_identity

F32 = mybir.dt.float32
BF16 = mybir.dt.bfloat16
I32 = mybir.dt.int32
U32 = mybir.dt.uint32
U16 = mybir.dt.uint16
U8 = mybir.dt.uint8
FP8X4 = mybir.dt.float8_e4m3fn_x4
ALU = mybir.AluOpType
ACT = mybir.ActivationFunctionType
AX = mybir.AxisListType

D, T, J, Q, E = 512, 2048, 512, 256, 512
P = 128
FLOPS = 2 * Q * J * D + 2 * E * Q * J


def tile_attend_cachemerge_pl_kernel(tc, query, keys, vals, ka, kb, va, vb, size, vsc, offs, offs2, out_0, out_1, out_2):
    nc = tc.nc
    with ExitStack() as ctx:
        lists = ctx.enter_context(tc.tile_pool(name="lists", bufs=1))
        keep = ctx.enter_context(tc.tile_pool(name="keep", bufs=1))
        turn = ctx.enter_context(tc.psum_pool(name="turn", bufs=6))
        prod = ctx.enter_context(tc.psum_pool(name="prod", bufs=2))

        def sbuf(shape, dtype, name, slot=None):
            return keep.tile(shape, dtype, name=name, tag=slot or name, align_bytes=64)

        kept = lists.tile([P, J // 16], U16, name="kept")
        evicted = lists.tile([P, J // 16], U16, name="evicted")
        key_pool = [sbuf([P, T], F32, "key_pool%d" % g) for g in range(4)]
        val_pool = [sbuf([P, T], F32, "val_pool%d" % t) for t in range(4)]
        q_raw = sbuf([P, 4, Q], F32, "q_raw")
        cols = {name: sbuf([P, 4], F32, "col_" + name) for name in ("ka", "kb", "va", "vb", "size", "vsc")}

        def load_col(queue, name, src):
            queue.dma_start(out=cols[name][:], in_=src.rearrange("o (p c) -> (o p) c", c=4))

        val_rows = vals.rearrange("(p t) n -> p t n", t=4)
        nc.sync.dma_start(kept[:], offs)
        load_col(nc.scalar, "ka", ka)
        nc.sync.dma_start(out=key_pool[0][:], in_=keys[0:P, :])
        load_col(nc.scalar, "kb", kb)
        nc.sync.dma_start(evicted[:], offs2)
        load_col(nc.scalar, "va", va)
        load_col(nc.scalar, "vb", vb)
        nc.scalar.dma_start(out=cols["vsc"][:], in_=vsc.rearrange("(p c) o -> p (c o)", c=4))
        load_col(nc.sync, "size", size)
        for g in range(1, 4):
            nc.sync.dma_start(out=key_pool[g][:], in_=keys[g * P : (g + 1) * P, :])
        nc.sync.dma_start(out=q_raw[:], in_=query.rearrange("(p t) q -> p t q", t=4))
        for t in range(4):
            nc.sync.dma_start(out=val_pool[t][:], in_=val_rows[:, t, :])

        ident = sbuf([P, P], F32, "ident")
        make_identity(nc, ident[:])

        def spread(col, names, pairs):
            bank = turn.tile([P, 4, P], F32, name="bank")
            for c in range(4):
                nc.tensor.transpose(bank[:, c, :], col[:, c : c + 1].to_broadcast([P, P]), ident[:])
            rows = [sbuf([P, J], F32, name) for name in names]
            for row in rows:
                if pairs:
                    nc.scalar.copy(out=row[:].rearrange("p (u n e) -> p u n e", u=2, e=2), in_=bank[:].rearrange("p (u e) n -> p u n e", u=2))
                else:
                    nc.scalar.copy(out=row[:].rearrange("p (n c) -> p n c", c=4), in_=bank[:].rearrange("p c n -> p n c"))
            return rows

        def gather(pool_tile, offsets, share, name, slot=None):
            picked = sbuf([P, J], F32, name, slot)
            nc.vector.tensor_tensor(picked[:], pool_tile[:].indirect(offsets[:]), share[:], ALU.mult)
            return picked

        def turn_and_add(bank, picked, columns, first):
            for c in range(4):
                nc.tensor.matmul(bank[:, c, :], picked[:, columns(c)], ident[:], start=(first and c == 0), stop=(not first and c == 3), is_transpose=True)

        def quantize(codes, scales, src):
            nc.vector.quantize_mx(out=codes.bitcast(FP8X4), scales=scales, in_=src)

        (ka_row,) = spread(cols["ka"], ["ka_row"], False)
        (kb_row,) = spread(cols["kb"], ["kb_row"], False)
        va_col = sbuf([P, 4], F32, "va_col")
        vb_col = sbuf([P, 4], F32, "vb_col")
        nc.gpsimd.tensor_tensor(va_col[:], cols["va"][:], cols["vsc"][:], ALU.mult)
        nc.gpsimd.tensor_tensor(vb_col[:], cols["vb"][:], cols["vsc"][:], ALU.mult)

        km_rows = sbuf([P, 4, 2, P, 2], BF16, "km_rows")

        def key_block(g):
            bank = turn.tile([P, 4, P], F32, name="bank")
            blocks = lambda c: slice(c * P, (c + 1) * P)
            turn_and_add(bank, gather(key_pool[g], kept, ka_row, "ka%d" % g), blocks, True)
            turn_and_add(bank, gather(key_pool[g], evicted, kb_row, "kb%d" % g), blocks, False)
            nc.scalar.copy(out=km_rows[:, :, :, 32 * g : 32 * (g + 1), :], in_=bank[:].rearrange("j c (r u e) -> j c u r e", u=2, e=2))

        key_block(0)
        va_rows = spread(va_col, ["va_row1", "va_row2", "va_row3"], False)
        (vb_row,) = spread(vb_col, ["vb_row"], False)
        (size_row,) = spread(cols["size"], ["size_row"], True)
        for g in range(1, 4):
            key_block(g)

        q_words = sbuf([P, Q, 4], BF16, "q_words")
        nc.scalar.copy(out=q_words[:], in_=q_raw[:].rearrange("p t q -> p q t"))
        q_codes = sbuf([P, Q], U32, "q_codes", "ka_row")
        q_scales = sbuf([P, Q], U8, "q_scales")
        quantize(q_codes[:], q_scales[:], q_words[:].rearrange("p q t -> p (q t)"))

        km_pairs = km_rows[:].rearrange("j c u p e -> j (c u p e)").bitcast(F32)
        km_words = sbuf([P, J * 4], BF16, "km_words")
        for b in range(2):
            bank = turn.tile([P, 2, 2, P], F32, name="bank")
            for c in range(2):
                for u in range(2):
                    at = ((2 * b + c) * 2 + u) * P
                    nc.tensor.transpose(bank[:, c, u, :], km_pairs[:, at : at + P], ident[:])
            nc.scalar.copy(
                out=km_words[:, 1024 * b : 1024 * (b + 1)].bitcast(F32).rearrange("p (c j u) -> p c j u", c=2, u=2),
                in_=bank[:].rearrange("p c u j -> p c j u"),
            )

        v_words = [sbuf([P, 2 * J], BF16, "v_words0")]
        steps = lambda s: slice(s, J, 4)

        def value_kept(t):
            bank = turn.tile([P, 4, P], F32, name="bank")
            turn_and_add(bank, gather(val_pool[t], kept, va_rows[max(t - 1, 0)], "va%d" % t), steps, True)
            return bank

        def value_evicted(t, bank, slot=None):
            turn_and_add(bank, gather(val_pool[t], evicted, vb_row, "vb%d" % t, slot), steps, False)

        def value_words(t, bank):
            words = v_words[t // 2][:, (t % 2) * J : (t % 2 + 1) * J]
            nc.scalar.copy(out=words.rearrange("p (e s) -> p e s", s=4), in_=bank[:].rearrange("p s e -> p e s"))

        for t in range(2):
            bank = value_kept(t)
            value_evicted(t, bank)
            value_words(t, bank)

        km_codes = sbuf([P, J], U32, "km_codes", "va_row1")
        km_scales = sbuf([P, J], U8, "km_scales")
        quantize(km_codes[:], km_scales[:], km_words[:])
        scores = [prod.tile([P, J], F32, name="product") for h in range(2)]
        for h in range(2):
            rows = slice(h * P, (h + 1) * P)
            nc.tensor.matmul_mx(out=scores[h][:], lhsT=q_codes[:, rows].bitcast(FP8X4), lhsT_scale=q_scales[:, rows], rhs=km_codes[:].bitcast(FP8X4), rhs_scale=km_scales[:], start=True, stop=True)

        third = value_kept(2)
        value_evicted(2, third)

        weights = []
        totals = sbuf([P, 2], F32, "totals")
        for h in range(2):
            neg_max = sbuf([P, 1], F32, "neg_max%d" % h, "va_row2" if h == 0 else None)
            nc.vector.tensor_reduce(out=neg_max[:], in_=scores[h][:], axis=AX.X, op=ALU.max, negate=True)
            p_rows = sbuf([P, J], F32, "p_rows%d" % h)
            nc.scalar.activation(out=p_rows[:].rearrange("q (u n e) -> q u n e", u=2, e=2), in_=scores[h][:].rearrange("q (n u e) -> q u n e", u=2, e=2), func=ACT.Exp, bias=neg_max[:], scale=1.0, accum_out=totals[:, h : h + 1])
            weights.append(p_rows)

        v_words.append(sbuf([P, 2 * J], BF16, "v_words1", "neg_max1"))
        value_words(2, third)
        bank = value_kept(3)
        inverse = sbuf([P, 2], F32, "inverse")
        nc.vector.reciprocal(inverse[:], totals[:])
        w_bank = turn.tile([P, 2, 2, P], F32, name="bank")
        for h in range(2):
            w_rows = sbuf([P, J], BF16, "w_rows%d" % h)
            nc.vector.scalar_tensor_tensor(out=w_rows[:], in0=weights[h][:], scalar=inverse[:, h : h + 1], in1=size_row[:], op0=ALU.mult, op1=ALU.mult)
            w_pairs = w_rows[:].bitcast(F32)
            for u in range(2):
                nc.tensor.transpose(w_bank[:, h, u, :], w_pairs[:, u * P : (u + 1) * P], ident[:])
        w_words = sbuf([P, Q * 4], BF16, "w_words")
        nc.scalar.copy(out=w_words[:].bitcast(F32).rearrange("p (h q u) -> p h q u", h=2, u=2), in_=w_bank[:].rearrange("p h u q -> p h q u"))

        value_evicted(3, bank, "p_rows0")
        value_words(3, bank)

        codes = sbuf([P, Q + E], U32, "codes", "val_pool3")
        w_scales = sbuf([P, Q], U8, "w_scales")
        v_scales = sbuf([P, E], U8, "v_scales")
        quantize(codes[:, 0:Q], w_scales[:], w_words[:])
        quantize(codes[:, Q : Q + 2 * P], v_scales[:, 0 : 2 * P], v_words[0][:])
        quantize(codes[:, Q + 2 * P : Q + 3 * P], v_scales[:, 2 * P : 3 * P], v_words[1][:, 0:J])
        result = [prod.tile([P, 4, P], F32, name="product") for h in range(2)]
        out_view = out_0.rearrange("(p t) q -> p t q", t=4)

        def product(t, h):
            rows = slice(h * P, (h + 1) * P)
            nc.tensor.matmul_mx(out=result[h][:, t, :], lhsT=codes[:, Q + t * P : Q + (t + 1) * P].bitcast(FP8X4), lhsT_scale=v_scales[:, t * P : (t + 1) * P], rhs=codes[:, rows].bitcast(FP8X4), rhs_scale=w_scales[:, rows], start=True, stop=True)

        out_rows = sbuf([P, 3, Q], F32, "out_rows")
        for h in range(2):
            for t in range(3):
                product(t, h)
        quantize(codes[:, Q + 3 * P : Q + 4 * P], v_scales[:, 3 * P : 4 * P], v_words[1][:, J : 2 * J])
        nc.scalar.copy(out=out_rows[:, :, 0:P], in_=result[0][:, 0:3, :])
        nc.vector.tensor_copy(out=out_rows[:, :, P:Q], in_=result[1][:, 0:3, :])
        nc.sync.dma_start(out=out_view[:, 0:3, :], in_=out_rows[:])
        for h in range(2):
            product(3, h)

        halves = [sbuf([P, P, 4], BF16, "out_words%d" % h) for h in range(2)]
        nc.vector.tensor_copy(out=halves[0][:], in_=result[0][:].rearrange("p t q -> p q t"))
        nc.scalar.copy(out=halves[1][:], in_=result[1][:].rearrange("p t q -> p q t"))
        last = sbuf([P, Q], F32, "last_rows")
        for h in range(2):
            nc.scalar.copy(out=last[:, h * P : (h + 1) * P], in_=result[h][:, 3, :])
        nc.scalar.dma_start(out=out_view[:, 3, :], in_=last[:])
        o_codes = sbuf([P, Q], U32, "o_codes")
        o_scales = sbuf([P, Q], U8, "o_scales")
        for h in range(2):
            rows = slice(h * P, (h + 1) * P)
            quantize(o_codes[:, rows], o_scales[:, rows], halves[h][:].rearrange("p q t -> p (q t)"))
        nc.sync.dma_start(out=out_1[0].rearrange("p q r -> p (q r)").bitcast(I32), in_=o_codes[:].bitcast(I32))
        for quad in range(4):
            queue = nc.sync if quad < 2 else nc.scalar
            queue.dma_start(out=out_2[0, 4 * quad : 4 * quad + 4, :].bitcast(I32), in_=o_scales[32 * quad : 32 * quad + 4, :].bitcast(I32))
